import numpy as np
import ml_dtypes


def mxq(x, axis, fmt="e4m3"):
    dtype, down = {"e4m3": (ml_dtypes.float8_e4m3fn, 7), "e5m2": (ml_dtypes.float8_e5m2, 14)}[fmt]
    v = np.moveaxis(np.asarray(x, np.float32).astype(ml_dtypes.bfloat16).astype(np.float64), axis, -1)
    blocks = v.reshape(v.shape[:-1] + (-1, 32))
    amax = np.abs(blocks).max(-1, keepdims=True)
    byte = np.maximum(np.where(amax > 0, np.frexp(amax)[1] - 1 + 127, 0) - down, 1)
    scale = np.exp2(byte - 127.0)
    codes = (blocks / scale).astype(np.float32).astype(dtype).astype(np.float64)
    return np.moveaxis((codes * scale).reshape(v.shape), -1, axis)


WIDE = False


def mx_kscale(k):
    if not WIDE:
        return np.ones(k)
    levels = np.array([10, -10, 5, -5, 0])
    if k % 512:
        return np.exp2(np.random.permutation(np.resize(levels, k // 32))).repeat(32)
    a = np.empty((k // 512, 16))
    for p in range(k // 512):
        a[p, :8] = np.random.permutation(np.resize(levels, 8))
        for g in range(8):
            far = levels[np.abs(levels - a[p, g]) >= 10]
            a[p, g + 8] = far[np.random.randint(len(far))]
    return np.exp2(a.ravel()).repeat(32)


def f64(x):
    return np.asarray(x).astype(np.float64)


def striped8(idx):
    return np.asarray(idx).reshape(8, -1, 16).transpose(0, 2, 1).reshape(128, -1).astype(np.uint16)


def unstriped8(offs):
    return offs.reshape(8, 16, -1).transpose(0, 2, 1).reshape(8, -1).astype(np.int64)


def pick8(x, idx, run):
    r = np.arange(len(x))
    return x[r[:, None], idx[r % (8 * run) // run]]


E2M1 = np.array([0.0, 0.5, 1.0, 1.5, 2.0, 3.0, 4.0, 6.0, -0.0, -0.5, -1.0, -1.5, -2.0, -3.0, -4.0, -6.0])


def pack_weight(w, fmt):
    k, n = w.shape
    w = f64(np.asarray(w, np.float32).astype(ml_dtypes.bfloat16)).reshape(k // 32, 32, n)
    amax = np.abs(w).max(1)
    if fmt == "e4m3":
        byte = np.frexp(amax)[1] - 1 + 127 - 7
    else:
        mant, ex = np.frexp(amax / 6.0)
        byte = np.where(mant > 0.5, ex, ex - 1) + 127
    byte = np.clip(np.where(amax > 0, byte, 1), 1, 254)
    scaled = (w * np.exp2(127.0 - byte)[:, None, :]).reshape(k, n).astype(np.float32)
    by_word = np.ascontiguousarray(scaled.reshape(k // 512, 128, 4, n).transpose(0, 1, 3, 2))
    if fmt == "e4m3":
        words = by_word.astype(ml_dtypes.float8_e4m3fn).view(np.uint8)
    else:
        c = by_word.astype(ml_dtypes.float4_e2m1fn).view(np.uint8) & 0xF
        words = (c[..., 0::2] | (c[..., 1::2] << 4)).reshape(k // 512, 128, 2 * n)
    return np.ascontiguousarray(words), np.ascontiguousarray(byte.astype(np.uint8).reshape(k // 512, 16, n))


def unpack_weight(words, scales, fmt):
    g, _, n = scales.shape
    words = np.ascontiguousarray(words).reshape(g, 128, n, -1)
    if fmt == "e4m3":
        vals = words.view(ml_dtypes.float8_e4m3fn).astype(np.float64)
    else:
        nib = np.empty((g, 128, n, 4), np.uint8)
        nib[..., 0::2] = words & 0xF
        nib[..., 1::2] = words >> 4
        vals = E2M1[nib]
    vals = vals * np.repeat(np.exp2(scales.astype(np.float64) - 127.0), 8, axis=1)[..., None]
    return vals.transpose(0, 1, 3, 2).reshape(g * 512, n)


D, T, U, I, Q = 512, 1024, 1024, 512, 128


def setup_inputs():
    n = np.random.standard_normal
    idx = np.stack([np.random.permutation(T)[:I] for _ in range(8)])
    idx2 = np.stack([np.random.permutation(U)[:I] for _ in range(8)])
    idx3 = np.stack([np.random.permutation(U)[:I] for _ in range(8)])
    fd = mx_kscale(D)
    keysp = pack_weight(n((D, T)) / fd[:, None], "e2m1")
    notesp = pack_weight(n((D, U)) / fd[:, None], "e4m3")
    return {
        "query": (n((D, Q)) * 1.0 / np.sqrt(D) * fd[:, None]).astype(np.float32),
        "keys_words": keysp[0],
        "keys_scales": keysp[1],
        "notes_words": notesp[0],
        "notes_scales": notesp[1],
        "lam": (np.random.uniform(2.0, 6.0, (Q, 1))).astype(np.float32),
        "offs": striped8(idx),
        "offs2": striped8(idx2),
        "offs3": striped8(idx3),
    }


def reference(query, keys_words, keys_scales, notes_words, notes_scales, lam, offs, offs2, offs3):
    idx = unstriped8(offs)
    idx2 = unstriped8(offs2)
    idx3 = unstriped8(offs3)
    keysu = unpack_weight(keys_words, keys_scales, "e2m1")
    notesu = unpack_weight(notes_words, notes_scales, "e4m3")
    queryq = mxq(f64(query), 0, "e4m3")
    a = queryq.T @ keysu
    b = queryq.T @ notesu
    ta = np.max(a, axis=1, keepdims=True)
    e1 = np.exp(pick8(a, idx, 16) - ta)
    f1 = np.zeros((Q, U))
    f1[np.arange(Q)[:, None], idx2[np.arange(Q) % 128 // 16]] = e1
    cc = b + f1 * f64(lam)
    tc2 = np.max(cc, axis=1, keepdims=True)
    y = np.exp(pick8(cc, idx3, 16) - tc2)
    return y

@@ -1,0 +1,142 @@
+from contextlib import ExitStack
+
+import concourse.mybir as mybir
+
+D, T, U, SLOTS, Q = 512, 1024, 1024, 512, 128
+FLOPS = 2 * D * Q * (T + U)
+
+F32 = mybir.dt.float32
+BF16 = mybir.dt.bfloat16
+I32 = mybir.dt.int32
+U32 = mybir.dt.uint32
+U16 = mybir.dt.uint16
+U8 = mybir.dt.uint8
+FP8X4 = mybir.dt.float8_e4m3fn_x4
+FP4X4 = mybir.dt.float4_e2m1fn_x4
+ALU = mybir.AluOpType
+EXP = mybir.ActivationFunctionType.Exp
+AXIS_X = mybir.AxisListType.X
+
+P = 128
+PACK = 4
+BANK = 512
+PIECE = 256
+LIST_ROWS = 16
+
+
+def load_scale_rows(queue, plane, scales):
+    for quadrant in range(4):
+        queue.dma_start(
+            out=plane[32 * quadrant : 32 * quadrant + 4, :].bitcast(I32),
+            in_=scales[0, 4 * quadrant : 4 * quadrant + 4, :].bitcast(I32),
+        )
+
+
+def tile_attend_votedwords_two_kernel(
+    tc, query, keys_words, keys_scales, notes_words, notes_scales, lam, offs, offs2, offs3, out
+):
+    nc = tc.nc
+    with ExitStack() as ctx:
+        sb = ctx.enter_context(tc.tile_pool(name="sb", bufs=1))
+        ps = ctx.enter_context(tc.psum_pool(name="ps", bufs=1))
+
+        token_list = sb.tile([P, SLOTS // LIST_ROWS], U16, name="token_list")
+        vote_list = sb.tile([P, SLOTS // LIST_ROWS], U16, name="vote_list")
+        note_list = sb.tile([P, SLOTS // LIST_ROWS], U16, name="note_list")
+        q_raw = sb.tile([P, PACK, Q], F32, name="q_raw")
+        key_codes = sb.tile([P, 2 * T], U8, name="key_codes", align_bytes=64)
+        key_plane = sb.tile([P, T], U8, name="key_plane", align_bytes=64)
+        note_codes = sb.tile([P, U], U32, name="note_codes", align_bytes=64)
+        note_plane = sb.tile([P, U], U8, name="note_plane", align_bytes=64)
+        lam_col = sb.tile([P, 1], F32, name="lam_col")
+        votes = sb.tile([P, U], F32, name="votes")
+
+        nc.vector.memset(key_plane[:].bitcast(I32), 0)
+        nc.gpsimd.memset(note_plane[:].bitcast(I32), 0)
+        nc.gpsimd.memset(votes[:], 0.0)
+
+        nc.sync.dma_start(out=q_raw[:], in_=query.rearrange("(p j) q -> p j q", j=PACK))
+        nc.sync.dma_start(out=key_codes[:].bitcast(I32), in_=keys_words[0].bitcast(I32))
+        load_scale_rows(nc.sync, key_plane, keys_scales)
+        nc.sync.dma_start(token_list[:], offs)
+        nc.sync.dma_start(vote_list[:], offs2)
+        nc.sync.dma_start(
+            out=note_codes[:].bitcast(I32),
+            in_=notes_words[0].rearrange("p n t -> p (n t)").bitcast(I32),
+        )
+        load_scale_rows(nc.sync, note_plane, notes_scales)
+        nc.sync.dma_start(out=lam_col[:], in_=lam)
+        nc.sync.dma_start(note_list[:], offs3)
+
+        q_grouped = sb.tile([P, Q, PACK], BF16, name="q_grouped", align_bytes=64)
+        nc.vector.tensor_copy(out=q_grouped[:], in_=q_raw[:].rearrange("p j q -> p q j"))
+        q_codes = sb.tile([P, Q], U32, name="q_codes", align_bytes=64)
+        q_plane = sb.tile([P, Q], U8, name="q_plane", align_bytes=64)
+        nc.vector.quantize_mx(
+            out=q_codes[:].bitcast(FP8X4), scales=q_plane[:], in_=q_grouped[:].rearrange("p q j -> p (q j)")
+        )
+
+        token_scores = sb.tile([P, T], F32, name="token_scores")
+        bank_max = sb.tile([P, T // BANK], F32, name="bank_max")
+        for h in range(T // BANK):
+            bank = ps.tile([P, BANK], F32, name=f"token_bank{h}")
+            nc.tensor.matmul_mx(
+                out=bank[:],
+                lhsT=q_codes[:].bitcast(FP8X4),
+                lhsT_scale=q_plane[:],
+                rhs=key_codes[:, 2 * h * BANK : 2 * (h + 1) * BANK].bitcast(FP4X4),
+                rhs_scale=key_plane[:, h * BANK : (h + 1) * BANK],
+                start=True,
+                stop=True,
+            )
+            nc.vector.tensor_scalar(
+                out=token_scores[:, h * BANK : (h + 1) * BANK],
+                in0=bank[:],
+                scalar1=1.0,
+                scalar2=None,
+                op0=ALU.mult,
+                op1=ALU.max,
+                accum_out=bank_max[:, h : h + 1],
+            )
+        neg_token_max = sb.tile([P, 1], F32, name="neg_token_max")
+        nc.vector.tensor_reduce(out=neg_token_max[:], in_=bank_max[:], axis=AXIS_X, op=ALU.max, negate=True)
+
+        note_banks = []
+        for h in range(U // BANK):
+            bank = ps.tile([P, BANK], F32, name=f"note_bank{h}")
+            nc.tensor.matmul_mx(
+                out=bank[:],
+                lhsT=q_codes[:].bitcast(FP8X4),
+                lhsT_scale=q_plane[:],
+                rhs=note_codes[:, h * BANK : (h + 1) * BANK].bitcast(FP8X4),
+                rhs_scale=note_plane[:, h * BANK : (h + 1) * BANK],
+                start=True,
+                stop=True,
+            )
+            note_banks.append(bank)
+
+        list_cols = PIECE // LIST_ROWS
+        for s in range(SLOTS // PIECE):
+            cols = slice(s * list_cols, (s + 1) * list_cols)
+            picked = sb.tile([P, PIECE], F32, name=f"picked{s}")
+            nc.scalar.activation(picked[:], token_scores[:].indirect(token_list[:, cols]), EXP, bias=neg_token_max[:])
+            nc.vector.tensor_copy(votes[:].indirect(vote_list[:, cols]), picked[:])
+
+        sums = sb.tile([P, U], F32, name="sums")
+        for h in range(U // BANK):
+            nc.vector.scalar_tensor_tensor(
+                out=sums[:, h * BANK : (h + 1) * BANK],
+                in0=votes[:, h * BANK : (h + 1) * BANK],
+                scalar=lam_col[:],
+                in1=note_banks[h][:],
+                op0=ALU.mult,
+                op1=ALU.add,
+            )
+        neg_sum_max = sb.tile([P, 1], F32, name="neg_sum_max")
+        nc.vector.tensor_reduce(out=neg_sum_max[:], in_=sums[:], axis=AXIS_X, op=ALU.max, negate=True)
+
+        for s in range(SLOTS // PIECE):
+            cols = slice(s * list_cols, (s + 1) * list_cols)
+            result = sb.tile([P, PIECE], F32, name=f"result{s}")
+            nc.scalar.activation(result[:], sums[:].indirect(note_list[:, cols]), EXP, bias=neg_sum_max[:])
+            nc.sync.dma_start(out=out[:, s * PIECE : (s + 1) * PIECE], in_=result[:])

@@ -22,6 +22,9 @@ PACK = 4
 BANK = 512
 PIECE = 256
 LIST_ROWS = 16
+SCORE_COLS = 256
+Q_VECTOR = 80
+U_VECTOR = 688
 
 
 def load_scale_rows(queue, plane, scales):
@@ -52,24 +55,27 @@ def tile_attend_votedwords_two_kernel(
         votes = sb.tile([P, U], F32, name="votes")
 
         nc.vector.memset(key_plane[:].bitcast(I32), 0)
-        nc.gpsimd.memset(note_plane[:].bitcast(I32), 0)
-        nc.gpsimd.memset(votes[:], 0.0)
+        nc.vector.memset(note_plane[:].bitcast(I32), 0)
+        nc.vector.memset(votes[:], 0.0)
 
         nc.sync.dma_start(out=q_raw[:], in_=query.rearrange("(p j) q -> p j q", j=PACK))
-        nc.sync.dma_start(out=key_codes[:].bitcast(I32), in_=keys_words[0].bitcast(I32))
+        nc.sync.dma_start(out=key_codes[:, :T].bitcast(I32), in_=keys_words[0, :, :T].bitcast(I32))
         load_scale_rows(nc.sync, key_plane, keys_scales)
+        nc.sync.dma_start(out=key_codes[:, T:].bitcast(I32), in_=keys_words[0, :, T:].bitcast(I32))
         nc.sync.dma_start(token_list[:], offs)
+        nc.sync.dma_start(out=lam_col[:], in_=lam)
         nc.sync.dma_start(vote_list[:], offs2)
         nc.sync.dma_start(
             out=note_codes[:].bitcast(I32),
             in_=notes_words[0].rearrange("p n t -> p (n t)").bitcast(I32),
         )
         load_scale_rows(nc.sync, note_plane, notes_scales)
-        nc.sync.dma_start(out=lam_col[:], in_=lam)
         nc.sync.dma_start(note_list[:], offs3)
 
         q_grouped = sb.tile([P, Q, PACK], BF16, name="q_grouped", align_bytes=64)
-        nc.vector.tensor_copy(out=q_grouped[:], in_=q_raw[:].rearrange("p j q -> p q j"))
+        q_by_column = q_raw[:].rearrange("p j q -> p q j")
+        nc.vector.tensor_copy(out=q_grouped[:, :Q_VECTOR, :], in_=q_by_column[:, :Q_VECTOR, :])
+        nc.scalar.copy(out=q_grouped[:, Q_VECTOR:, :], in_=q_by_column[:, Q_VECTOR:, :])
         q_codes = sb.tile([P, Q], U32, name="q_codes", align_bytes=64)
         q_plane = sb.tile([P, Q], U8, name="q_plane", align_bytes=64)
         nc.vector.quantize_mx(
@@ -77,20 +83,20 @@ def tile_attend_votedwords_two_kernel(
         )
 
         token_scores = sb.tile([P, T], F32, name="token_scores")
-        bank_max = sb.tile([P, T // BANK], F32, name="bank_max")
-        for h in range(T // BANK):
-            bank = ps.tile([P, BANK], F32, name=f"token_bank{h}")
+        bank_max = sb.tile([P, T // SCORE_COLS], F32, name="bank_max")
+        for h in range(T // SCORE_COLS):
+            bank = ps.tile([P, SCORE_COLS], F32, name=f"token_bank{h}")
             nc.tensor.matmul_mx(
                 out=bank[:],
                 lhsT=q_codes[:].bitcast(FP8X4),
                 lhsT_scale=q_plane[:],
-                rhs=key_codes[:, 2 * h * BANK : 2 * (h + 1) * BANK].bitcast(FP4X4),
-                rhs_scale=key_plane[:, h * BANK : (h + 1) * BANK],
+                rhs=key_codes[:, 2 * h * SCORE_COLS : 2 * (h + 1) * SCORE_COLS].bitcast(FP4X4),
+                rhs_scale=key_plane[:, h * SCORE_COLS : (h + 1) * SCORE_COLS],
                 start=True,
                 stop=True,
             )
             nc.vector.tensor_scalar(
-                out=token_scores[:, h * BANK : (h + 1) * BANK],
+                out=token_scores[:, h * SCORE_COLS : (h + 1) * SCORE_COLS],
                 in0=bank[:],
                 scalar1=1.0,
                 scalar2=None,
@@ -115,23 +121,24 @@ def tile_attend_votedwords_two_kernel(
             )
             note_banks.append(bank)
 
+        lam_wide = sb.tile([P, PIECE], F32, name="lam_wide")
+        nc.scalar.copy(out=lam_wide[:], in_=lam_col[:].to_broadcast([P, PIECE]))
+        note_tail = sb.tile([P, U - U_VECTOR], F32, name="note_tail")
+        nc.scalar.copy(out=note_tail[:], in_=note_banks[1][:, U_VECTOR - BANK :])
+
         list_cols = PIECE // LIST_ROWS
         for s in range(SLOTS // PIECE):
             cols = slice(s * list_cols, (s + 1) * list_cols)
             picked = sb.tile([P, PIECE], F32, name=f"picked{s}")
             nc.scalar.activation(picked[:], token_scores[:].indirect(token_list[:, cols]), EXP, bias=neg_token_max[:])
-            nc.vector.tensor_copy(votes[:].indirect(vote_list[:, cols]), picked[:])
+            nc.vector.tensor_tensor(votes[:].indirect(vote_list[:, cols]), picked[:], lam_wide[:], ALU.mult)
 
         sums = sb.tile([P, U], F32, name="sums")
-        for h in range(U // BANK):
-            nc.vector.scalar_tensor_tensor(
-                out=sums[:, h * BANK : (h + 1) * BANK],
-                in0=votes[:, h * BANK : (h + 1) * BANK],
-                scalar=lam_col[:],
-                in1=note_banks[h][:],
-                op0=ALU.mult,
-                op1=ALU.add,
-            )
+        nc.gpsimd.tensor_tensor(sums[:, U_VECTOR:], votes[:, U_VECTOR:], note_tail[:], ALU.add)
+        nc.vector.tensor_tensor(sums[:, :BANK], votes[:, :BANK], note_banks[0][:], ALU.add)
+        nc.vector.tensor_tensor(
+            sums[:, BANK:U_VECTOR], votes[:, BANK:U_VECTOR], note_banks[1][:, : U_VECTOR - BANK], ALU.add
+        )
         neg_sum_max = sb.tile([P, 1], F32, name="neg_sum_max")
         nc.vector.tensor_reduce(out=neg_sum_max[:], in_=sums[:], axis=AXIS_X, op=ALU.max, negate=True)
 

@@ -23,7 +23,7 @@ BANK = 512
 PIECE = 256
 LIST_ROWS = 16
 SCORE_COLS = 256
-Q_VECTOR = 80
+Q_VECTOR = 64
 U_VECTOR = 688
 
 
@@ -59,9 +59,9 @@ def tile_attend_votedwords_two_kernel(
         nc.vector.memset(votes[:], 0.0)
 
         nc.sync.dma_start(out=q_raw[:], in_=query.rearrange("(p j) q -> p j q", j=PACK))
-        nc.sync.dma_start(out=key_codes[:, :T].bitcast(I32), in_=keys_words[0, :, :T].bitcast(I32))
+        nc.sync.dma_start(out=key_codes[:, :2 * SCORE_COLS].bitcast(I32), in_=keys_words[0, :, :2 * SCORE_COLS].bitcast(I32))
         load_scale_rows(nc.sync, key_plane, keys_scales)
-        nc.sync.dma_start(out=key_codes[:, T:].bitcast(I32), in_=keys_words[0, :, T:].bitcast(I32))
+        nc.sync.dma_start(out=key_codes[:, 2 * SCORE_COLS:].bitcast(I32), in_=keys_words[0, :, 2 * SCORE_COLS:].bitcast(I32))
         nc.sync.dma_start(token_list[:], offs)
         nc.sync.dma_start(out=lam_col[:], in_=lam)
         nc.sync.dma_start(vote_list[:], offs2)
@@ -73,9 +73,10 @@ def tile_attend_votedwords_two_kernel(
         nc.sync.dma_start(note_list[:], offs3)
 
         q_grouped = sb.tile([P, Q, PACK], BF16, name="q_grouped", align_bytes=64)
-        q_by_column = q_raw[:].rearrange("p j q -> p q j")
-        nc.vector.tensor_copy(out=q_grouped[:, :Q_VECTOR, :], in_=q_by_column[:, :Q_VECTOR, :])
-        nc.scalar.copy(out=q_grouped[:, Q_VECTOR:, :], in_=q_by_column[:, Q_VECTOR:, :])
+        q_source = q_raw[:].rearrange("p j (c i) -> p c j i", i=4)
+        q_target = q_grouped[:].rearrange("p (c i) j -> p c j i", i=4)
+        nc.vector.tensor_copy(out=q_target[:, : Q_VECTOR // 4], in_=q_source[:, : Q_VECTOR // 4])
+        nc.scalar.copy(out=q_target[:, Q_VECTOR // 4 :], in_=q_source[:, Q_VECTOR // 4 :])
         q_codes = sb.tile([P, Q], U32, name="q_codes", align_bytes=64)
         q_plane = sb.tile([P, Q], U8, name="q_plane", align_bytes=64)
         nc.vector.quantize_mx(

@@ -62,8 +62,8 @@ def tile_attend_votedwords_two_kernel(
         nc.sync.dma_start(out=key_codes[:, :2 * SCORE_COLS].bitcast(I32), in_=keys_words[0, :, :2 * SCORE_COLS].bitcast(I32))
         load_scale_rows(nc.sync, key_plane, keys_scales)
         nc.sync.dma_start(out=key_codes[:, 2 * SCORE_COLS:].bitcast(I32), in_=keys_words[0, :, 2 * SCORE_COLS:].bitcast(I32))
-        nc.sync.dma_start(token_list[:], offs)
         nc.sync.dma_start(out=lam_col[:], in_=lam)
+        nc.sync.dma_start(token_list[:], offs)
         nc.sync.dma_start(vote_list[:], offs2)
         nc.sync.dma_start(
             out=note_codes[:].bitcast(I32),
@@ -96,15 +96,20 @@ def tile_attend_votedwords_two_kernel(
                 start=True,
                 stop=True,
             )
-            nc.vector.tensor_scalar(
-                out=token_scores[:, h * SCORE_COLS : (h + 1) * SCORE_COLS],
-                in0=bank[:],
-                scalar1=1.0,
-                scalar2=None,
-                op0=ALU.mult,
-                op1=ALU.max,
-                accum_out=bank_max[:, h : h + 1],
-            )
+            scores = token_scores[:, h * SCORE_COLS : (h + 1) * SCORE_COLS]
+            if h < T // SCORE_COLS - 1:
+                nc.vector.tensor_reduce(out=bank_max[:, h : h + 1], in_=bank[:], axis=AXIS_X, op=ALU.max)
+                nc.scalar.copy(out=scores, in_=bank[:])
+            else:
+                nc.vector.tensor_scalar(
+                    out=scores,
+                    in0=bank[:],
+                    scalar1=1.0,
+                    scalar2=None,
+                    op0=ALU.mult,
+                    op1=ALU.max,
+                    accum_out=bank_max[:, h : h + 1],
+                )
         neg_token_max = sb.tile([P, 1], F32, name="neg_token_max")
         nc.vector.tensor_reduce(out=neg_token_max[:], in_=bank_max[:], axis=AXIS_X, op=ALU.max, negate=True)
 

from contextlib import ExitStack

import concourse.mybir as mybir

D, T, U, SLOTS, Q = 512, 1024, 1024, 512, 128
FLOPS = 2 * D * Q * (T + U)

F32 = mybir.dt.float32
BF16 = mybir.dt.bfloat16
I32 = mybir.dt.int32
U32 = mybir.dt.uint32
U16 = mybir.dt.uint16
U8 = mybir.dt.uint8
FP8X4 = mybir.dt.float8_e4m3fn_x4
FP4X4 = mybir.dt.float4_e2m1fn_x4
ALU = mybir.AluOpType
EXP = mybir.ActivationFunctionType.Exp
AXIS_X = mybir.AxisListType.X

P = 128
PACK = 4
BANK = 512
PIECE = 256
LIST_ROWS = 16
SCORE_COLS = 256
Q_VECTOR = 64
U_VECTOR = 688


def load_scale_rows(queue, plane, scales):
    for quadrant in range(4):
        queue.dma_start(
            out=plane[32 * quadrant : 32 * quadrant + 4, :].bitcast(I32),
            in_=scales[0, 4 * quadrant : 4 * quadrant + 4, :].bitcast(I32),
        )


def tile_attend_votedwords_two_kernel(
    tc, query, keys_words, keys_scales, notes_words, notes_scales, lam, offs, offs2, offs3, out
):
    nc = tc.nc
    with ExitStack() as ctx:
        sb = ctx.enter_context(tc.tile_pool(name="sb", bufs=1))
        ps = ctx.enter_context(tc.psum_pool(name="ps", bufs=1))

        token_list = sb.tile([P, SLOTS // LIST_ROWS], U16, name="token_list")
        vote_list = sb.tile([P, SLOTS // LIST_ROWS], U16, name="vote_list")
        note_list = sb.tile([P, SLOTS // LIST_ROWS], U16, name="note_list")
        q_raw = sb.tile([P, PACK, Q], F32, name="q_raw")
        key_codes = sb.tile([P, 2 * T], U8, name="key_codes", align_bytes=64)
        key_plane = sb.tile([P, T], U8, name="key_plane", align_bytes=64)
        note_codes = sb.tile([P, U], U32, name="note_codes", align_bytes=64)
        note_plane = sb.tile([P, U], U8, name="note_plane", align_bytes=64)
        lam_col = sb.tile([P, 1], F32, name="lam_col")
        votes = sb.tile([P, U], F32, name="votes")

        nc.vector.memset(key_plane[:].bitcast(I32), 0)
        nc.vector.memset(note_plane[:].bitcast(I32), 0)
        nc.vector.memset(votes[:], 0.0)

        nc.sync.dma_start(out=q_raw[:], in_=query.rearrange("(p j) q -> p j q", j=PACK))
        nc.sync.dma_start(out=key_codes[:, :2 * SCORE_COLS].bitcast(I32), in_=keys_words[0, :, :2 * SCORE_COLS].bitcast(I32))
        load_scale_rows(nc.sync, key_plane, keys_scales)
        nc.sync.dma_start(out=key_codes[:, 2 * SCORE_COLS:].bitcast(I32), in_=keys_words[0, :, 2 * SCORE_COLS:].bitcast(I32))
        nc.sync.dma_start(out=lam_col[:], in_=lam)
        nc.sync.dma_start(token_list[:], offs)
        nc.sync.dma_start(vote_list[:], offs2)
        nc.sync.dma_start(
            out=note_codes[:].bitcast(I32),
            in_=notes_words[0].rearrange("p n t -> p (n t)").bitcast(I32),
        )
        load_scale_rows(nc.sync, note_plane, notes_scales)
        nc.sync.dma_start(note_list[:], offs3)

        q_grouped = sb.tile([P, Q, PACK], BF16, name="q_grouped", align_bytes=64)
        q_source = q_raw[:].rearrange("p j (c i) -> p c j i", i=4)
        q_target = q_grouped[:].rearrange("p (c i) j -> p c j i", i=4)
        nc.vector.tensor_copy(out=q_target[:, : Q_VECTOR // 4], in_=q_source[:, : Q_VECTOR // 4])
        nc.scalar.copy(out=q_target[:, Q_VECTOR // 4 :], in_=q_source[:, Q_VECTOR // 4 :])
        q_codes = sb.tile([P, Q], U32, name="q_codes", align_bytes=64)
        q_plane = sb.tile([P, Q], U8, name="q_plane", align_bytes=64)
        nc.vector.quantize_mx(
            out=q_codes[:].bitcast(FP8X4), scales=q_plane[:], in_=q_grouped[:].rearrange("p q j -> p (q j)")
        )

        token_scores = sb.tile([P, T], F32, name="token_scores")
        bank_max = sb.tile([P, T // SCORE_COLS], F32, name="bank_max")
        for h in range(T // SCORE_COLS):
            bank = ps.tile([P, SCORE_COLS], F32, name=f"token_bank{h}")
            nc.tensor.matmul_mx(
                out=bank[:],
                lhsT=q_codes[:].bitcast(FP8X4),
                lhsT_scale=q_plane[:],
                rhs=key_codes[:, 2 * h * SCORE_COLS : 2 * (h + 1) * SCORE_COLS].bitcast(FP4X4),
                rhs_scale=key_plane[:, h * SCORE_COLS : (h + 1) * SCORE_COLS],
                start=True,
                stop=True,
            )
            scores = token_scores[:, h * SCORE_COLS : (h + 1) * SCORE_COLS]
            if h < T // SCORE_COLS - 1:
                nc.vector.tensor_reduce(out=bank_max[:, h : h + 1], in_=bank[:], axis=AXIS_X, op=ALU.max)
                nc.scalar.copy(out=scores, in_=bank[:])
            else:
                nc.vector.tensor_scalar(
                    out=scores,
                    in0=bank[:],
                    scalar1=1.0,
                    scalar2=None,
                    op0=ALU.mult,
                    op1=ALU.max,
                    accum_out=bank_max[:, h : h + 1],
                )
        neg_token_max = sb.tile([P, 1], F32, name="neg_token_max")
        nc.vector.tensor_reduce(out=neg_token_max[:], in_=bank_max[:], axis=AXIS_X, op=ALU.max, negate=True)

        note_banks = []
        for h in range(U // BANK):
            bank = ps.tile([P, BANK], F32, name=f"note_bank{h}")
            nc.tensor.matmul_mx(
                out=bank[:],
                lhsT=q_codes[:].bitcast(FP8X4),
                lhsT_scale=q_plane[:],
                rhs=note_codes[:, h * BANK : (h + 1) * BANK].bitcast(FP8X4),
                rhs_scale=note_plane[:, h * BANK : (h + 1) * BANK],
                start=True,
                stop=True,
            )
            note_banks.append(bank)

        lam_wide = sb.tile([P, PIECE], F32, name="lam_wide")
        nc.scalar.copy(out=lam_wide[:], in_=lam_col[:].to_broadcast([P, PIECE]))
        note_tail = sb.tile([P, U - U_VECTOR], F32, name="note_tail")
        nc.scalar.copy(out=note_tail[:], in_=note_banks[1][:, U_VECTOR - BANK :])

        list_cols = PIECE // LIST_ROWS
        for s in range(SLOTS // PIECE):
            cols = slice(s * list_cols, (s + 1) * list_cols)
            picked = sb.tile([P, PIECE], F32, name=f"picked{s}")
            nc.scalar.activation(picked[:], token_scores[:].indirect(token_list[:, cols]), EXP, bias=neg_token_max[:])
            nc.vector.tensor_tensor(votes[:].indirect(vote_list[:, cols]), picked[:], lam_wide[:], ALU.mult)

        sums = sb.tile([P, U], F32, name="sums")
        nc.gpsimd.tensor_tensor(sums[:, U_VECTOR:], votes[:, U_VECTOR:], note_tail[:], ALU.add)
        nc.vector.tensor_tensor(sums[:, :BANK], votes[:, :BANK], note_banks[0][:], ALU.add)
        nc.vector.tensor_tensor(
            sums[:, BANK:U_VECTOR], votes[:, BANK:U_VECTOR], note_banks[1][:, : U_VECTOR - BANK], ALU.add
        )
        neg_sum_max = sb.tile([P, 1], F32, name="neg_sum_max")
        nc.vector.tensor_reduce(out=neg_sum_max[:], in_=sums[:], axis=AXIS_X, op=ALU.max, negate=True)

        for s in range(SLOTS // PIECE):
            cols = slice(s * list_cols, (s + 1) * list_cols)
            result = sb.tile([P, PIECE], F32, name=f"result{s}")
            nc.scalar.activation(result[:], sums[:].indirect(note_list[:, cols]), EXP, bias=neg_sum_max[:])
            nc.sync.dma_start(out=out[:, s * PIECE : (s + 1) * PIECE], in_=result[:])
